import numpy as np
import ml_dtypes


def mxq(x, axis, fmt="e4m3"):
    dtype, down = {"e4m3": (ml_dtypes.float8_e4m3fn, 7), "e5m2": (ml_dtypes.float8_e5m2, 14)}[fmt]
    v = np.moveaxis(np.asarray(x, np.float32).astype(ml_dtypes.bfloat16).astype(np.float64), axis, -1)
    blocks = v.reshape(v.shape[:-1] + (-1, 32))
    amax = np.abs(blocks).max(-1, keepdims=True)
    byte = np.maximum(np.where(amax > 0, np.frexp(amax)[1] - 1 + 127, 0) - down, 1)
    scale = np.exp2(byte - 127.0)
    codes = (blocks / scale).astype(np.float32).astype(dtype).astype(np.float64)
    return np.moveaxis((codes * scale).reshape(v.shape), -1, axis)


WIDE = False


def mx_kscale(k):
    if not WIDE:
        return np.ones(k)
    levels = np.array([10, -10, 5, -5, 0])
    if k % 512:
        return np.exp2(np.random.permutation(np.resize(levels, k // 32))).repeat(32)
    a = np.empty((k // 512, 16))
    for p in range(k // 512):
        a[p, :8] = np.random.permutation(np.resize(levels, 8))
        for g in range(8):
            far = levels[np.abs(levels - a[p, g]) >= 10]
            a[p, g + 8] = far[np.random.randint(len(far))]
    return np.exp2(a.ravel()).repeat(32)


def f64(x):
    return np.asarray(x).astype(np.float64)


def striped(idx):
    return np.tile(idx.reshape(-1, 16).T, (8, 1)).astype(np.uint16)


def unstriped(offs):
    return offs[:16].T.reshape(-1).astype(np.int64)


def pack_weight(w):
    k, n = w.shape
    w = f64(np.asarray(w, np.float32).astype(ml_dtypes.bfloat16)).reshape(k // 32, 32, n)
    amax = np.abs(w).max(1)
    byte = np.clip(np.where(amax > 0, np.frexp(amax)[1] - 1 + 127 - 7, 1), 1, 254)
    scaled = (w * np.exp2(127.0 - byte)[:, None, :]).reshape(k, n).astype(np.float32)
    words = np.ascontiguousarray(scaled.reshape(k // 512, 128, 4, n).transpose(0, 1, 3, 2)).astype(ml_dtypes.float8_e4m3fn).view(np.uint8)
    return words, np.ascontiguousarray(byte.astype(np.uint8).reshape(k // 512, 16, n))


def unpack_weight(words, scales):
    g, p, n, _ = words.shape
    vals = np.ascontiguousarray(words).view(ml_dtypes.float8_e4m3fn).astype(np.float64) * np.repeat(np.exp2(scales.astype(np.float64) - 127.0), 8, axis=1)[..., None]
    return vals.transpose(0, 1, 3, 2).reshape(g * 512, n)


K, T, S, D, N = 512, 4096, 1024, 8, 256


def setup_inputs():
    n = np.random.standard_normal
    s = mx_kscale(K)[:, None]
    packed_xT = pack_weight(n((K, T)) * s)
    return {
        "x_words": packed_xT[0],
        "x_scales": packed_xT[1],
        "w1": (n((K, N)) / np.sqrt(K) / s).astype(np.float32),
        "w2": (n((K, N)) / np.sqrt(K) / s).astype(np.float32),
        "ca": (-0.5 * n((N, 1))).astype(np.float32),
        "thb": (-0.5 * n((N, 1))).astype(np.float32),
        "offs": striped(np.random.permutation(T)[:S]),
    }


def reference(x_words, x_scales, w1, w2, ca, thb, offs):
    xq = unpack_weight(x_words, x_scales)[:, unstriped(offs)]
    a0 = (mxq(f64(w1), 0, "e4m3").T @ xq) + f64(ca)
    b0 = (mxq(f64(w2), 0, "e4m3").T @ xq) + f64(thb)
    b6 = b0 + 6.0
    e1 = np.maximum(b6, np.pad(b6, ((0, 0), (0, 1)))[:, 1:])
    imp = np.maximum(-1.0 * a0, np.maximum(e1, np.pad(e1, ((0, 0), (0, 2)))[:, 2:]) - 6.0)
    ex = np.exp(-2.0 * imp)
    return -0.5 * (np.log(ex.reshape(len(ex), -1, D).mean(axis=2)))

@@ -1,0 +1,162 @@
+from contextlib import ExitStack
+
+import concourse.mybir as mybir
+
+K, T, S, D, N = 512, 4096, 1024, 8, 256
+FLOPS = 2 * 2 * K * N * S
+
+F32 = mybir.dt.float32
+BF16 = mybir.dt.bfloat16
+I32 = mybir.dt.int32
+U32 = mybir.dt.uint32
+U16 = mybir.dt.uint16
+U8 = mybir.dt.uint8
+FP8X4 = mybir.dt.float8_e4m3fn_x4
+ALU = mybir.AluOpType
+ACT = mybir.ActivationFunctionType
+AXIS_X = mybir.AxisListType.X
+
+P = 128
+PACK = 4
+HALF = 512
+ROW_TILES = N // P
+HALVES = S // HALF
+GROUPS = S // D
+LIST_COLS = HALF // 16
+
+
+def tile_picked_ystl_soft_p_kernel(tc, x_words, x_scales, w1, w2, ca, thb, offs, out):
+    nc = tc.nc
+    with ExitStack() as ctx:
+        keep = ctx.enter_context(tc.tile_pool(name="keep", bufs=1))
+        psum = ctx.enter_context(tc.psum_pool(name="psum", bufs=1))
+
+        offsets = keep.tile([P, S // 16], U16, name="offsets")
+        nc.sync.dma_start(offsets[:], offs)
+
+        table_words = keep.tile([P, T], I32, name="table_words")
+        nc.sync.dma_start(table_words[:], x_words[0].rearrange("p n t -> p (n t)").bitcast(I32))
+
+        table_scales = keep.tile([P, T], U8, name="table_scales")
+        nc.vector.memset(table_scales[:].bitcast(I32), 0)
+        for q in range(4):
+            nc.scalar.dma_start(table_scales[32 * q : 32 * q + 4, :].bitcast(I32), x_scales[0, 4 * q : 4 * q + 4, :].bitcast(I32))
+
+        raw = {}
+        for name, w in (("b", w2), ("a", w1)):
+            raw[name] = keep.tile([P, PACK, N], F32, name="raw_" + name)
+            nc.sync.dma_start(raw[name][:], w.rearrange("(p j) m -> p j m", j=PACK))
+
+        ca_sb = keep.tile([P, ROW_TILES], F32, name="ca_sb")
+        thb_sb = keep.tile([P, ROW_TILES], F32, name="thb_sb")
+        with nc.allow_non_contiguous_dma(reason="one threshold a partition"):
+            nc.gpsimd.dma_start(thb_sb[:], thb.rearrange("(r p) o -> p (r o)", p=P))
+            nc.gpsimd.dma_start(ca_sb[:], ca.rearrange("(r p) o -> p (r o)", p=P))
+        neg_thb = keep.tile([P, ROW_TILES], F32, name="neg_thb")
+        nc.scalar.mul(neg_thb[:], thb_sb[:], -1.0)
+
+        neg_b = [keep.tile([P, S + 8], F32, name="neg_b%d" % r) for r in range(ROW_TILES)]
+        pair = [keep.tile([P, S + 8], F32, name="pair%d" % r) for r in range(ROW_TILES)]
+        for r in range(ROW_TILES):
+            nc.gpsimd.memset(neg_b[r][:, S:], 6.0)
+            nc.gpsimd.memset(pair[r][:, S:], 6.0)
+
+        x_bytes = keep.tile([P, S], U8, name="x_bytes", align_bytes=64)
+        nc.vector.tensor_copy(x_bytes[:], table_scales[:].indirect(offsets[:]))
+        x_codes = [keep.tile([P, HALF], U32, name="x_codes%d" % h, align_bytes=64) for h in range(HALVES)]
+        for h in range(HALVES):
+            nc.vector.tensor_copy(x_codes[h][:], table_words[:].bitcast(U32).indirect(offsets[:, h * LIST_COLS : (h + 1) * LIST_COLS]))
+
+        sums = {}
+
+        def products(name, r):
+            grouped = keep.tile([P, P, PACK], BF16, name="grouped_%s%d" % (name, r), align_bytes=64)
+            nc.scalar.copy(grouped[:], raw[name][:, :, r * P : (r + 1) * P].rearrange("p j m -> p m j"))
+            codes = keep.tile([P, P], U32, name="codes_%s%d" % (name, r), align_bytes=64)
+            scales = keep.tile([P, P], U8, name="scales_%s%d" % (name, r), align_bytes=64)
+            nc.vector.quantize_mx(out=codes[:].bitcast(FP8X4), scales=scales[:], in_=grouped[:].rearrange("p m j -> p (m j)"))
+            for h in range(HALVES):
+                acc = psum.tile([P, HALF], F32, name="acc_%s%d%d" % (name, r, h))
+                nc.tensor.matmul_mx(
+                    out=acc[:],
+                    lhsT=codes[:].bitcast(FP8X4),
+                    lhsT_scale=scales[:],
+                    rhs=x_codes[h][:].bitcast(FP8X4),
+                    rhs_scale=x_bytes[:, h * HALF : (h + 1) * HALF],
+                    start=True,
+                    stop=True,
+                )
+                sums[name, r, h] = acc
+
+        window = [keep.tile([P, S], F32, name="window%d" % r) for r in range(ROW_TILES)]
+        neg_imp = [keep.tile([P, S], F32, name="neg_imp%d" % r) for r in range(ROW_TILES)]
+        shifted = [keep.tile([P, S], F32, name="shifted%d" % r) for r in range(ROW_TILES)]
+        ex = [keep.tile([P, S], F32, name="ex%d" % r) for r in range(ROW_TILES)]
+        peak = keep.tile([P, ROW_TILES, GROUPS], F32, name="peak")
+        total = keep.tile([P, ROW_TILES, GROUPS], F32, name="total")
+
+        def by_group(ap):
+            return ap.rearrange("p (v d) -> p v d", d=D)
+
+        def negate_b(r, h):
+            nc.scalar.activation(neg_b[r][:, h * HALF : (h + 1) * HALF], sums["b", r, h][:], ACT.Identity, bias=neg_thb[:, r : r + 1], scale=-1.0)
+
+        def least_of_two(r, lo, hi):
+            nc.vector.tensor_tensor(pair[r][:, lo:hi], neg_b[r][:, lo:hi], neg_b[r][:, lo + 1 : hi + 1], ALU.min)
+
+        def least_of_four(r, lo, hi):
+            nc.vector.tensor_tensor(window[r][:, lo:hi], pair[r][:, lo:hi], pair[r][:, lo + 2 : hi + 2], ALU.min)
+
+        def implication(r, h):
+            cols = slice(h * HALF, (h + 1) * HALF)
+            nc.vector.scalar_tensor_tensor(neg_imp[r][:, cols], sums["a", r, h][:], ca_sb[:, r : r + 1], window[r][:, cols], ALU.add, ALU.min)
+
+        def group_peak(r, lo, hi):
+            nc.vector.tensor_reduce(peak[:, r, lo // D : hi // D], by_group(neg_imp[r][:, lo:hi]), AXIS_X, ALU.max)
+
+        def shift_and_exp(engine, r, lo, hi):
+            engine.tensor_tensor(
+                by_group(shifted[r][:, lo:hi]),
+                by_group(neg_imp[r][:, lo:hi]),
+                peak[:, r, lo // D : hi // D].unsqueeze(2).to_broadcast([P, (hi - lo) // D, D]),
+                ALU.subtract,
+            )
+            nc.scalar.activation(ex[r][:, lo:hi], shifted[r][:, lo:hi], ACT.Exp, scale=2.0)
+
+        def group_total(r, lo, hi):
+            nc.vector.tensor_reduce(total[:, r, lo // D : hi // D], by_group(ex[r][:, lo:hi]), AXIS_X, ALU.add)
+
+        products("b", 0)
+        products("b", 1)
+        products("a", 0)
+        for r in range(ROW_TILES):
+            for h in range(HALVES):
+                negate_b(r, h)
+        products("a", 1)
+
+        least_of_two(0, 0, HALF - 1)
+        least_of_two(0, HALF - 1, S)
+        least_of_four(0, 0, HALF - 3)
+        least_of_two(1, 0, HALF - 1)
+        least_of_four(0, HALF - 3, S)
+        least_of_two(1, HALF - 1, S)
+        implication(0, 0)
+        least_of_four(1, 0, S)
+        implication(0, 1)
+        implication(1, 0)
+        group_peak(0, 0, S)
+        implication(1, 1)
+        shift_and_exp(nc.vector, 0, 0, S)
+        group_peak(1, 0, HALF)
+        group_peak(1, HALF, S)
+        shift_and_exp(nc.vector, 1, 0, HALF)
+        shift_and_exp(nc.vector, 1, HALF, S)
+        group_total(0, 0, S)
+        group_total(1, 0, HALF)
+        group_total(1, HALF, S)
+
+        log_mean = keep.tile([P, ROW_TILES, GROUPS], F32, name="log_mean")
+        nc.scalar.activation(log_mean[:], total[:], ACT.Ln, scale=1.0 / D)
+        result = keep.tile([P, ROW_TILES, GROUPS], F32, name="result")
+        nc.vector.scalar_tensor_tensor(result[:], log_mean[:], -0.5, peak[:], ALU.mult, ALU.subtract)
+        nc.sync.dma_start(out.rearrange("(r p) v -> p r v", p=P), result[:])

@@ -34,18 +34,16 @@ def tile_picked_ystl_soft_p_kernel(tc, x_words, x_scales, w1, w2, ca, thb, offs,
         offsets = keep.tile([P, S // 16], U16, name="offsets")
         nc.sync.dma_start(offsets[:], offs)
 
-        table_words = keep.tile([P, T], I32, name="table_words")
-        nc.sync.dma_start(table_words[:], x_words[0].rearrange("p n t -> p (n t)").bitcast(I32))
+        raw = {name: keep.tile([P, PACK, N], F32, name="raw_" + name) for name in "ab"}
+        nc.sync.dma_start(raw["b"][:], w2.rearrange("(p j) m -> p j m", j=PACK))
 
         table_scales = keep.tile([P, T], U8, name="table_scales")
         nc.vector.memset(table_scales[:].bitcast(I32), 0)
-        for q in range(4):
-            nc.scalar.dma_start(table_scales[32 * q : 32 * q + 4, :].bitcast(I32), x_scales[0, 4 * q : 4 * q + 4, :].bitcast(I32))
+        nc.sync.dma_start(table_scales[0:P:8, :].bitcast(I32), x_scales[0].bitcast(I32))
 
-        raw = {}
-        for name, w in (("b", w2), ("a", w1)):
-            raw[name] = keep.tile([P, PACK, N], F32, name="raw_" + name)
-            nc.sync.dma_start(raw[name][:], w.rearrange("(p j) m -> p j m", j=PACK))
+        table_words = keep.tile([P, T], I32, name="table_words")
+        nc.sync.dma_start(table_words[:], x_words[0].rearrange("p n t -> p (n t)").bitcast(I32))
+        nc.sync.dma_start(raw["a"][:], w1.rearrange("(p j) m -> p j m", j=PACK))
 
         ca_sb = keep.tile([P, ROW_TILES], F32, name="ca_sb")
         thb_sb = keep.tile([P, ROW_TILES], F32, name="thb_sb")
@@ -62,7 +60,11 @@ def tile_picked_ystl_soft_p_kernel(tc, x_words, x_scales, w1, w2, ca, thb, offs,
             nc.gpsimd.memset(pair[r][:, S:], 6.0)
 
         x_bytes = keep.tile([P, S], U8, name="x_bytes", align_bytes=64)
-        nc.vector.tensor_copy(x_bytes[:], table_scales[:].indirect(offsets[:]))
+        nc.gpsimd.memset(x_bytes[:].bitcast(I32), 0)
+        picked_bytes = keep.tile([P, S], U8, name="picked_bytes")
+        nc.vector.tensor_copy(picked_bytes[:], table_scales[:].indirect(offsets[:]))
+        for q in range(4):
+            nc.scalar.dma_start(x_bytes[32 * q : 32 * q + 4, :].bitcast(I32), picked_bytes[32 * q : 32 * q + 32 : 8, :].bitcast(I32))
         x_codes = [keep.tile([P, HALF], U32, name="x_codes%d" % h, align_bytes=64) for h in range(HALVES)]
         for h in range(HALVES):
             nc.vector.tensor_copy(x_codes[h][:], table_words[:].bitcast(U32).indirect(offsets[:, h * LIST_COLS : (h + 1) * LIST_COLS]))
@@ -151,12 +153,17 @@ def tile_picked_ystl_soft_p_kernel(tc, x_words, x_scales, w1, w2, ca, thb, offs,
         group_peak(1, HALF, S)
         shift_and_exp(nc.vector, 1, 0, HALF)
         shift_and_exp(nc.vector, 1, HALF, S)
-        group_total(0, 0, S)
+        group_total(0, 0, HALF)
+        group_total(0, HALF, S)
         group_total(1, 0, HALF)
         group_total(1, HALF, S)
 
         log_mean = keep.tile([P, ROW_TILES, GROUPS], F32, name="log_mean")
-        nc.scalar.activation(log_mean[:], total[:], ACT.Ln, scale=1.0 / D)
+        flat_total = total[:].rearrange("p r v -> p (r v)")
+        flat_log = log_mean[:].rearrange("p r v -> p (r v)")
+        first = HALF // D
+        nc.scalar.activation(flat_log[:, :first], flat_total[:, :first], ACT.Ln, scale=1.0 / D)
+        nc.scalar.activation(flat_log[:, first:], flat_total[:, first:], ACT.Ln, scale=1.0 / D)
         result = keep.tile([P, ROW_TILES, GROUPS], F32, name="result")
         nc.vector.scalar_tensor_tensor(result[:], log_mean[:], -0.5, peak[:], ALU.mult, ALU.subtract)
         nc.sync.dma_start(out.rearrange("(r p) v -> p r v", p=P), result[:])

@@ -1,6 +1,7 @@
 from contextlib import ExitStack
 
 import concourse.mybir as mybir
+from concourse.masks import make_identity
 
 K, T, S, D, N = 512, 4096, 1024, 8, 256
 FLOPS = 2 * 2 * K * N * S
@@ -48,54 +49,62 @@ def tile_picked_ystl_soft_p_kernel(tc, x_words, x_scales, w1, w2, ca, thb, offs,
         ca_sb = keep.tile([P, ROW_TILES], F32, name="ca_sb")
         thb_sb = keep.tile([P, ROW_TILES], F32, name="thb_sb")
         with nc.allow_non_contiguous_dma(reason="one threshold a partition"):
-            nc.gpsimd.dma_start(thb_sb[:], thb.rearrange("(r p) o -> p (r o)", p=P))
-            nc.gpsimd.dma_start(ca_sb[:], ca.rearrange("(r p) o -> p (r o)", p=P))
+            nc.scalar.dma_start(thb_sb[:], thb.rearrange("(r p) o -> p (r o)", p=P))
+            nc.scalar.dma_start(ca_sb[:], ca.rearrange("(r p) o -> p (r o)", p=P))
         neg_thb = keep.tile([P, ROW_TILES], F32, name="neg_thb")
         nc.scalar.mul(neg_thb[:], thb_sb[:], -1.0)
 
-        neg_b = [keep.tile([P, S + 8], F32, name="neg_b%d" % r) for r in range(ROW_TILES)]
+        neg_b = [keep.tile([P, S + 8], F32, name="neg_b%d" % r, tag="neg_b%d" % r, align_bytes=64) for r in range(ROW_TILES)]
         pair = [keep.tile([P, S + 8], F32, name="pair%d" % r) for r in range(ROW_TILES)]
         for r in range(ROW_TILES):
             nc.gpsimd.memset(neg_b[r][:, S:], 6.0)
             nc.gpsimd.memset(pair[r][:, S:], 6.0)
 
-        x_bytes = keep.tile([P, S], U8, name="x_bytes", align_bytes=64)
-        nc.gpsimd.memset(x_bytes[:].bitcast(I32), 0)
-        picked_bytes = keep.tile([P, S], U8, name="picked_bytes")
-        nc.vector.tensor_copy(picked_bytes[:], table_scales[:].indirect(offsets[:]))
-        for q in range(4):
-            nc.scalar.dma_start(x_bytes[32 * q : 32 * q + 4, :].bitcast(I32), picked_bytes[32 * q : 32 * q + 32 : 8, :].bitcast(I32))
+        x_bytes = [keep.tile([P, HALF], U8, name="x_bytes%d" % h, align_bytes=64) for h in range(HALVES)]
+        for h in range(HALVES):
+            picked = keep.tile([P, HALF], U8, name="picked%d" % h)
+            nc.vector.tensor_copy(picked[:], table_scales[:].indirect(offsets[:, h * LIST_COLS : (h + 1) * LIST_COLS]))
+            nc.vector.tensor_copy(x_bytes[h][:].bitcast(I32), picked[:].bitcast(I32))
+            for i in range(1, 4):
+                nc.scalar.dma_start(x_bytes[h][i:P:32, :].bitcast(I32), picked[8 * i : P : 32, :].bitcast(I32))
         x_codes = [keep.tile([P, HALF], U32, name="x_codes%d" % h, align_bytes=64) for h in range(HALVES)]
         for h in range(HALVES):
             nc.vector.tensor_copy(x_codes[h][:], table_words[:].bitcast(U32).indirect(offsets[:, h * LIST_COLS : (h + 1) * LIST_COLS]))
 
+        weights = {}
         sums = {}
 
-        def products(name, r):
-            grouped = keep.tile([P, P, PACK], BF16, name="grouped_%s%d" % (name, r), align_bytes=64)
+        def quantize(name, r, tag):
+            grouped = keep.tile([P, P, PACK], BF16, name="grouped_%s%d" % (name, r), tag=tag, align_bytes=64)
             nc.scalar.copy(grouped[:], raw[name][:, :, r * P : (r + 1) * P].rearrange("p j m -> p m j"))
             codes = keep.tile([P, P], U32, name="codes_%s%d" % (name, r), align_bytes=64)
             scales = keep.tile([P, P], U8, name="scales_%s%d" % (name, r), align_bytes=64)
             nc.vector.quantize_mx(out=codes[:].bitcast(FP8X4), scales=scales[:], in_=grouped[:].rearrange("p m j -> p (m j)"))
-            for h in range(HALVES):
-                acc = psum.tile([P, HALF], F32, name="acc_%s%d%d" % (name, r, h))
-                nc.tensor.matmul_mx(
-                    out=acc[:],
-                    lhsT=codes[:].bitcast(FP8X4),
-                    lhsT_scale=scales[:],
-                    rhs=x_codes[h][:].bitcast(FP8X4),
-                    rhs_scale=x_bytes[:, h * HALF : (h + 1) * HALF],
-                    start=True,
-                    stop=True,
-                )
-                sums[name, r, h] = acc
+            weights[name, r] = (codes, scales)
+
+        def product(name, r, h):
+            codes, scales = weights[name, r]
+            acc = psum.tile([P, HALF], F32, name="acc_%s%d%d" % (name, r, h), tag="bank_%s%d%d" % (name, r, h))
+            nc.tensor.matmul_mx(
+                out=acc[:],
+                lhsT=codes[:].bitcast(FP8X4),
+                lhsT_scale=scales[:],
+                rhs=x_codes[h][:].bitcast(FP8X4),
+                rhs_scale=x_bytes[h][:],
+                start=True,
+                stop=True,
+            )
+            sums[name, r, h] = acc
+
+        identity = keep.tile([P, P], F32, name="identity")
+        make_identity(nc, identity[:])
 
         window = [keep.tile([P, S], F32, name="window%d" % r) for r in range(ROW_TILES)]
         neg_imp = [keep.tile([P, S], F32, name="neg_imp%d" % r) for r in range(ROW_TILES)]
-        shifted = [keep.tile([P, S], F32, name="shifted%d" % r) for r in range(ROW_TILES)]
+        shifted = keep.tile([P, S], F32, name="shifted")
         ex = [keep.tile([P, S], F32, name="ex%d" % r) for r in range(ROW_TILES)]
-        peak = keep.tile([P, ROW_TILES, GROUPS], F32, name="peak")
-        total = keep.tile([P, ROW_TILES, GROUPS], F32, name="total")
+        least = keep.tile([P, ROW_TILES, GROUPS], F32, name="least")
+        total = keep.tile([P, GROUPS], F32, name="total")
 
         def by_group(ap):
             return ap.rearrange("p (v d) -> p v d", d=D)
@@ -113,57 +122,78 @@ def tile_picked_ystl_soft_p_kernel(tc, x_words, x_scales, w1, w2, ca, thb, offs,
             cols = slice(h * HALF, (h + 1) * HALF)
             nc.vector.scalar_tensor_tensor(neg_imp[r][:, cols], sums["a", r, h][:], ca_sb[:, r : r + 1], window[r][:, cols], ALU.add, ALU.min)
 
-        def group_peak(r, lo, hi):
-            nc.vector.tensor_reduce(peak[:, r, lo // D : hi // D], by_group(neg_imp[r][:, lo:hi]), AXIS_X, ALU.max)
+        def group_least(r, lo, hi):
+            nc.vector.tensor_reduce(least[:, r, lo // D : hi // D], by_group(neg_imp[r][:, lo:hi]), AXIS_X, ALU.max, negate=True)
 
-        def shift_and_exp(engine, r, lo, hi):
-            engine.tensor_tensor(
-                by_group(shifted[r][:, lo:hi]),
-                by_group(neg_imp[r][:, lo:hi]),
-                peak[:, r, lo // D : hi // D].unsqueeze(2).to_broadcast([P, (hi - lo) // D, D]),
-                ALU.subtract,
+        def shift_and_exp(lo, hi):
+            nc.vector.tensor_tensor(
+                by_group(shifted[:, lo:hi]),
+                by_group(neg_imp[1][:, lo:hi]),
+                least[:, 1, lo // D : hi // D].unsqueeze(2).to_broadcast([P, (hi - lo) // D, D]),
+                ALU.add,
             )
-            nc.scalar.activation(ex[r][:, lo:hi], shifted[r][:, lo:hi], ACT.Exp, scale=2.0)
+            nc.scalar.activation(ex[1][:, lo:hi], shifted[:, lo:hi], ACT.Exp, scale=2.0)
 
-        def group_total(r, lo, hi):
-            nc.vector.tensor_reduce(total[:, r, lo // D : hi // D], by_group(ex[r][:, lo:hi]), AXIS_X, ALU.add)
+        def group_total(lo, hi):
+            nc.vector.tensor_reduce(total[:, lo // D : hi // D], by_group(ex[1][:, lo:hi]), AXIS_X, ALU.add)
 
-        products("b", 0)
-        products("b", 1)
-        products("a", 0)
-        for r in range(ROW_TILES):
-            for h in range(HALVES):
+        def first_tile_on_tensor():
+            free_banks = ("bank_b00", "bank_b01", "bank_b10", "bank_b11")
+            per_bank = D // len(free_banks)
+            for k, tag in enumerate(free_banks):
+                turned = psum.tile([P, per_bank, P], F32, name="turned%d" % k, tag=tag)
+                for i in range(per_bank):
+                    d = k * per_bank + i
+                    nc.tensor.matmul(turned[:, i, :], neg_imp[0][:, d:S:D], identity[:], start=True, stop=False, is_transpose=True)
+                    nc.tensor.matmul(turned[:, i, :], least[:, 0, :], identity[:], start=False, stop=True, is_transpose=True)
+                cols = slice(k * per_bank * P, (k + 1) * per_bank * P)
+                nc.scalar.activation(ex[0][:, cols], turned[:].rearrange("p i m -> p (i m)"), ACT.Exp, scale=2.0)
+            summed = psum.tile([P, GROUPS], F32, name="summed", tag="bank_a00")
+            for d in range(D):
+                nc.tensor.matmul(summed[:], ex[0][:, d * P : (d + 1) * P], identity[:], start=(d == 0), stop=(d == D - 1), is_transpose=True)
+            return summed
+
+        quantize("b", 0, "grouped_b0")
+        quantize("b", 1, "grouped_b1")
+        quantize("a", 0, "grouped_a0")
+        for h in range(HALVES):
+            for r in range(ROW_TILES):
+                product("b", r, h)
                 negate_b(r, h)
-        products("a", 1)
+        for h in range(HALVES):
+            product("a", 0, h)
 
+        quarter = HALF // 2
         least_of_two(0, 0, HALF - 1)
-        least_of_two(0, HALF - 1, S)
-        least_of_four(0, 0, HALF - 3)
         least_of_two(1, 0, HALF - 1)
+        least_of_two(0, HALF - 1, S)
+        quantize("a", 1, "neg_b0")
+        for h in range(HALVES):
+            product("a", 1, h)
+        least_of_four(0, 0, HALF - 3)
         least_of_four(0, HALF - 3, S)
         least_of_two(1, HALF - 1, S)
         implication(0, 0)
-        least_of_four(1, 0, S)
         implication(0, 1)
+        group_least(0, 0, HALF)
+        group_least(0, HALF, S)
+        summed = first_tile_on_tensor()
+        least_of_four(1, 0, HALF)
+        least_of_four(1, HALF, S)
         implication(1, 0)
-        group_peak(0, 0, S)
         implication(1, 1)
-        shift_and_exp(nc.vector, 0, 0, S)
-        group_peak(1, 0, HALF)
-        group_peak(1, HALF, S)
-        shift_and_exp(nc.vector, 1, 0, HALF)
-        shift_and_exp(nc.vector, 1, HALF, S)
-        group_total(0, 0, HALF)
-        group_total(0, HALF, S)
-        group_total(1, 0, HALF)
-        group_total(1, HALF, S)
+        group_least(1, 0, HALF)
+        group_least(1, HALF, HALF + quarter)
+        shift_and_exp(0, HALF)
+        group_least(1, HALF + quarter, S)
+        shift_and_exp(HALF, HALF + quarter)
+        shift_and_exp(HALF + quarter, S)
+        group_total(0, HALF)
+        group_total(HALF, S)
 
-        log_mean = keep.tile([P, ROW_TILES, GROUPS], F32, name="log_mean")
-        flat_total = total[:].rearrange("p r v -> p (r v)")
-        flat_log = log_mean[:].rearrange("p r v -> p (r v)")
-        first = HALF // D
-        nc.scalar.activation(flat_log[:, :first], flat_total[:, :first], ACT.Ln, scale=1.0 / D)
-        nc.scalar.activation(flat_log[:, first:], flat_total[:, first:], ACT.Ln, scale=1.0 / D)
+        log_mean = shifted[:, S - ROW_TILES * GROUPS :].rearrange("p (r v) -> p r v", r=ROW_TILES)
         result = keep.tile([P, ROW_TILES, GROUPS], F32, name="result")
-        nc.vector.scalar_tensor_tensor(result[:], log_mean[:], -0.5, peak[:], ALU.mult, ALU.subtract)
-        nc.sync.dma_start(out.rearrange("(r p) v -> p r v", p=P), result[:])
+        for r, group_sums in enumerate((summed, total)):
+            nc.scalar.activation(log_mean[:, r, :], group_sums[:], ACT.Ln, scale=1.0 / D)
+            nc.vector.scalar_tensor_tensor(result[:, r, :], log_mean[:, r, :], -0.5, least[:, r, :], ALU.mult, ALU.add)
+            nc.sync.dma_start(out[r * P : (r + 1) * P, :], result[:, r, :])

from contextlib import ExitStack

import concourse.mybir as mybir
from concourse.masks import make_identity

K, T, S, D, N = 512, 4096, 1024, 8, 256
FLOPS = 2 * 2 * K * N * S

F32 = mybir.dt.float32
BF16 = mybir.dt.bfloat16
I32 = mybir.dt.int32
U32 = mybir.dt.uint32
U16 = mybir.dt.uint16
U8 = mybir.dt.uint8
FP8X4 = mybir.dt.float8_e4m3fn_x4
ALU = mybir.AluOpType
ACT = mybir.ActivationFunctionType
AXIS_X = mybir.AxisListType.X

P = 128
PACK = 4
HALF = 512
ROW_TILES = N // P
HALVES = S // HALF
GROUPS = S // D
LIST_COLS = HALF // 16


def tile_picked_ystl_soft_p_kernel(tc, x_words, x_scales, w1, w2, ca, thb, offs, out):
    nc = tc.nc
    with ExitStack() as ctx:
        keep = ctx.enter_context(tc.tile_pool(name="keep", bufs=1))
        psum = ctx.enter_context(tc.psum_pool(name="psum", bufs=1))

        offsets = keep.tile([P, S // 16], U16, name="offsets")
        nc.sync.dma_start(offsets[:], offs)

        raw = {name: keep.tile([P, PACK, N], F32, name="raw_" + name) for name in "ab"}
        nc.sync.dma_start(raw["b"][:], w2.rearrange("(p j) m -> p j m", j=PACK))

        table_scales = keep.tile([P, T], U8, name="table_scales")
        nc.vector.memset(table_scales[:].bitcast(I32), 0)
        nc.sync.dma_start(table_scales[0:P:8, :].bitcast(I32), x_scales[0].bitcast(I32))

        table_words = keep.tile([P, T], I32, name="table_words")
        nc.sync.dma_start(table_words[:], x_words[0].rearrange("p n t -> p (n t)").bitcast(I32))
        nc.sync.dma_start(raw["a"][:], w1.rearrange("(p j) m -> p j m", j=PACK))

        ca_sb = keep.tile([P, ROW_TILES], F32, name="ca_sb")
        thb_sb = keep.tile([P, ROW_TILES], F32, name="thb_sb")
        with nc.allow_non_contiguous_dma(reason="one threshold a partition"):
            nc.scalar.dma_start(thb_sb[:], thb.rearrange("(r p) o -> p (r o)", p=P))
            nc.scalar.dma_start(ca_sb[:], ca.rearrange("(r p) o -> p (r o)", p=P))
        neg_thb = keep.tile([P, ROW_TILES], F32, name="neg_thb")
        nc.scalar.mul(neg_thb[:], thb_sb[:], -1.0)

        neg_b = [keep.tile([P, S + 8], F32, name="neg_b%d" % r, tag="neg_b%d" % r, align_bytes=64) for r in range(ROW_TILES)]
        pair = [keep.tile([P, S + 8], F32, name="pair%d" % r) for r in range(ROW_TILES)]
        for r in range(ROW_TILES):
            nc.gpsimd.memset(neg_b[r][:, S:], 6.0)
            nc.gpsimd.memset(pair[r][:, S:], 6.0)

        x_bytes = [keep.tile([P, HALF], U8, name="x_bytes%d" % h, align_bytes=64) for h in range(HALVES)]
        for h in range(HALVES):
            picked = keep.tile([P, HALF], U8, name="picked%d" % h)
            nc.vector.tensor_copy(picked[:], table_scales[:].indirect(offsets[:, h * LIST_COLS : (h + 1) * LIST_COLS]))
            nc.vector.tensor_copy(x_bytes[h][:].bitcast(I32), picked[:].bitcast(I32))
            for i in range(1, 4):
                nc.scalar.dma_start(x_bytes[h][i:P:32, :].bitcast(I32), picked[8 * i : P : 32, :].bitcast(I32))
        x_codes = [keep.tile([P, HALF], U32, name="x_codes%d" % h, align_bytes=64) for h in range(HALVES)]
        for h in range(HALVES):
            nc.vector.tensor_copy(x_codes[h][:], table_words[:].bitcast(U32).indirect(offsets[:, h * LIST_COLS : (h + 1) * LIST_COLS]))

        weights = {}
        sums = {}

        def quantize(name, r, tag):
            grouped = keep.tile([P, P, PACK], BF16, name="grouped_%s%d" % (name, r), tag=tag, align_bytes=64)
            nc.scalar.copy(grouped[:], raw[name][:, :, r * P : (r + 1) * P].rearrange("p j m -> p m j"))
            codes = keep.tile([P, P], U32, name="codes_%s%d" % (name, r), align_bytes=64)
            scales = keep.tile([P, P], U8, name="scales_%s%d" % (name, r), align_bytes=64)
            nc.vector.quantize_mx(out=codes[:].bitcast(FP8X4), scales=scales[:], in_=grouped[:].rearrange("p m j -> p (m j)"))
            weights[name, r] = (codes, scales)

        def product(name, r, h):
            codes, scales = weights[name, r]
            acc = psum.tile([P, HALF], F32, name="acc_%s%d%d" % (name, r, h), tag="bank_%s%d%d" % (name, r, h))
            nc.tensor.matmul_mx(
                out=acc[:],
                lhsT=codes[:].bitcast(FP8X4),
                lhsT_scale=scales[:],
                rhs=x_codes[h][:].bitcast(FP8X4),
                rhs_scale=x_bytes[h][:],
                start=True,
                stop=True,
            )
            sums[name, r, h] = acc

        identity = keep.tile([P, P], F32, name="identity")
        make_identity(nc, identity[:])

        window = [keep.tile([P, S], F32, name="window%d" % r) for r in range(ROW_TILES)]
        neg_imp = [keep.tile([P, S], F32, name="neg_imp%d" % r) for r in range(ROW_TILES)]
        shifted = keep.tile([P, S], F32, name="shifted")
        ex = [keep.tile([P, S], F32, name="ex%d" % r) for r in range(ROW_TILES)]
        least = keep.tile([P, ROW_TILES, GROUPS], F32, name="least")
        total = keep.tile([P, GROUPS], F32, name="total")

        def by_group(ap):
            return ap.rearrange("p (v d) -> p v d", d=D)

        def negate_b(r, h):
            nc.scalar.activation(neg_b[r][:, h * HALF : (h + 1) * HALF], sums["b", r, h][:], ACT.Identity, bias=neg_thb[:, r : r + 1], scale=-1.0)

        def least_of_two(r, lo, hi):
            nc.vector.tensor_tensor(pair[r][:, lo:hi], neg_b[r][:, lo:hi], neg_b[r][:, lo + 1 : hi + 1], ALU.min)

        def least_of_four(r, lo, hi):
            nc.vector.tensor_tensor(window[r][:, lo:hi], pair[r][:, lo:hi], pair[r][:, lo + 2 : hi + 2], ALU.min)

        def implication(r, h):
            cols = slice(h * HALF, (h + 1) * HALF)
            nc.vector.scalar_tensor_tensor(neg_imp[r][:, cols], sums["a", r, h][:], ca_sb[:, r : r + 1], window[r][:, cols], ALU.add, ALU.min)

        def group_least(r, lo, hi):
            nc.vector.tensor_reduce(least[:, r, lo // D : hi // D], by_group(neg_imp[r][:, lo:hi]), AXIS_X, ALU.max, negate=True)

        def shift_and_exp(lo, hi):
            nc.vector.tensor_tensor(
                by_group(shifted[:, lo:hi]),
                by_group(neg_imp[1][:, lo:hi]),
                least[:, 1, lo // D : hi // D].unsqueeze(2).to_broadcast([P, (hi - lo) // D, D]),
                ALU.add,
            )
            nc.scalar.activation(ex[1][:, lo:hi], shifted[:, lo:hi], ACT.Exp, scale=2.0)

        def group_total(lo, hi):
            nc.vector.tensor_reduce(total[:, lo // D : hi // D], by_group(ex[1][:, lo:hi]), AXIS_X, ALU.add)

        def first_tile_on_tensor():
            free_banks = ("bank_b00", "bank_b01", "bank_b10", "bank_b11")
            per_bank = D // len(free_banks)
            for k, tag in enumerate(free_banks):
                turned = psum.tile([P, per_bank, P], F32, name="turned%d" % k, tag=tag)
                for i in range(per_bank):
                    d = k * per_bank + i
                    nc.tensor.matmul(turned[:, i, :], neg_imp[0][:, d:S:D], identity[:], start=True, stop=False, is_transpose=True)
                    nc.tensor.matmul(turned[:, i, :], least[:, 0, :], identity[:], start=False, stop=True, is_transpose=True)
                cols = slice(k * per_bank * P, (k + 1) * per_bank * P)
                nc.scalar.activation(ex[0][:, cols], turned[:].rearrange("p i m -> p (i m)"), ACT.Exp, scale=2.0)
            summed = psum.tile([P, GROUPS], F32, name="summed", tag="bank_a00")
            for d in range(D):
                nc.tensor.matmul(summed[:], ex[0][:, d * P : (d + 1) * P], identity[:], start=(d == 0), stop=(d == D - 1), is_transpose=True)
            return summed

        quantize("b", 0, "grouped_b0")
        quantize("b", 1, "grouped_b1")
        quantize("a", 0, "grouped_a0")
        for h in range(HALVES):
            for r in range(ROW_TILES):
                product("b", r, h)
                negate_b(r, h)
        for h in range(HALVES):
            product("a", 0, h)

        quarter = HALF // 2
        least_of_two(0, 0, HALF - 1)
        least_of_two(1, 0, HALF - 1)
        least_of_two(0, HALF - 1, S)
        quantize("a", 1, "neg_b0")
        for h in range(HALVES):
            product("a", 1, h)
        least_of_four(0, 0, HALF - 3)
        least_of_four(0, HALF - 3, S)
        least_of_two(1, HALF - 1, S)
        implication(0, 0)
        implication(0, 1)
        group_least(0, 0, HALF)
        group_least(0, HALF, S)
        summed = first_tile_on_tensor()
        least_of_four(1, 0, HALF)
        least_of_four(1, HALF, S)
        implication(1, 0)
        implication(1, 1)
        group_least(1, 0, HALF)
        group_least(1, HALF, HALF + quarter)
        shift_and_exp(0, HALF)
        group_least(1, HALF + quarter, S)
        shift_and_exp(HALF, HALF + quarter)
        shift_and_exp(HALF + quarter, S)
        group_total(0, HALF)
        group_total(HALF, S)

        log_mean = shifted[:, S - ROW_TILES * GROUPS :].rearrange("p (r v) -> p r v", r=ROW_TILES)
        result = keep.tile([P, ROW_TILES, GROUPS], F32, name="result")
        for r, group_sums in enumerate((summed, total)):
            nc.scalar.activation(log_mean[:, r, :], group_sums[:], ACT.Ln, scale=1.0 / D)
            nc.vector.scalar_tensor_tensor(result[:, r, :], log_mean[:, r, :], -0.5, least[:, r, :], ALU.mult, ALU.add)
            nc.sync.dma_start(out[r * P : (r + 1) * P, :], result[:, r, :])
